import numpy as np
import ml_dtypes


def mxq(x, axis, fmt="e4m3"):
    dtype, down = {"e4m3": (ml_dtypes.float8_e4m3fn, 7), "e5m2": (ml_dtypes.float8_e5m2, 14)}[fmt]
    v = np.moveaxis(np.asarray(x, np.float32).astype(ml_dtypes.bfloat16).astype(np.float64), axis, -1)
    blocks = v.reshape(v.shape[:-1] + (-1, 32))
    amax = np.abs(blocks).max(-1, keepdims=True)
    byte = np.maximum(np.where(amax > 0, np.frexp(amax)[1] - 1 + 127, 0) - down, 1)
    scale = np.exp2(byte - 127.0)
    codes = (blocks / scale).astype(np.float32).astype(dtype).astype(np.float64)
    return np.moveaxis((codes * scale).reshape(v.shape), -1, axis)


WIDE = False


def mx_kscale(k):
    if not WIDE:
        return np.ones(k)
    levels = np.array([10, -10, 5, -5, 0])
    if k % 512:
        return np.exp2(np.random.permutation(np.resize(levels, k // 32))).repeat(32)
    a = np.empty((k // 512, 16))
    for p in range(k // 512):
        a[p, :8] = np.random.permutation(np.resize(levels, 8))
        for g in range(8):
            far = levels[np.abs(levels - a[p, g]) >= 10]
            a[p, g + 8] = far[np.random.randint(len(far))]
    return np.exp2(a.ravel()).repeat(32)


def f64(x):
    return np.asarray(x).astype(np.float64)


def striped(idx):
    return np.tile(np.asarray(idx).reshape(-1, 16).T, (8, 1)).astype(np.uint16)


def unstriped(offs):
    return offs[:16].T.reshape(-1).astype(np.int64)


O, G, T, D, M = 4, 1024, 512, 512, 256


def setup_inputs():
    n = np.random.standard_normal
    s = mx_kscale(D)[:, None]
    grid = lambda x: np.round(x * 32) / 32
    return {
        "cb": (grid(n((O, D, T))) / s).astype(np.float32),
        "w": (n((D, M)) * s / np.sqrt(O * D)).astype(np.float32),
        "norm": np.tile(np.random.randint(32, 129, G) / 64.0, (128, 1)).astype(np.float32),
        "bias": (0.3 * n((M, 1))).astype(np.float32),
        "offs": striped(np.random.randint(0, T, O * G)),
    }


def reference(cb, w, norm, bias, offs):
    code = unstriped(offs).reshape(O, G)
    e = sum(f64(cb)[o][:, code[o]] for o in range(O)) * f64(norm)[:1]
    y = mxq(f64(w), 0, "e4m3").T @ mxq(e, 0, "e4m3")
    y = y + f64(bias)
    return y

@@ -1,0 +1,154 @@
+from contextlib import ExitStack
+
+import concourse.mybir as mybir
+
+O, G, T, D, M = 4, 1024, 512, 512, 256
+P = 128
+PACK = 4
+PAIRS = 2
+CHUNK = 256
+CHUNKS = G // CHUNK
+FLOPS = 2 * D * M * G
+
+F32 = mybir.dt.float32
+BF16 = mybir.dt.bfloat16
+U32 = mybir.dt.uint32
+U16 = mybir.dt.uint16
+U8 = mybir.dt.uint8
+FP8X4 = mybir.dt.float8_e4m3fn_x4
+ADD = mybir.AluOpType.add
+MULT = mybir.AluOpType.mult
+COPY = mybir.ActivationFunctionType.Copy
+IDENTITY = mybir.ActivationFunctionType.Identity
+
+
+def tile_attend_aq_bias_kernel(tc, cb, w, norm, bias, offs, out):
+    nc = tc.nc
+    with ExitStack() as ctx:
+        lists = ctx.enter_context(tc.tile_pool(name="lists", bufs=1))
+        keep = ctx.enter_context(tc.tile_pool(name="keep", bufs=1))
+        psum = ctx.enter_context(tc.psum_pool(name="psum", bufs=1))
+
+        def raw_view(o, h):
+            return cb[o].rearrange("(p t) c -> p t c", t=PACK)[:, 2 * h : 2 * h + 2, :]
+
+        raws = {}
+        tabs = {}
+        half = T // 2
+        offsets = lists.tile([P, O * G // 16], U16, name="offsets")
+        first = [keep.tile([P, 2, half], F32, name=f"raw_first{i}") for i in range(2)]
+        nc.sync.dma_start(out=first[0][:], in_=raw_view(0, 0)[:, :, 0:half])
+        nc.sync.dma_start(out=first[1][:], in_=raw_view(0, 0)[:, :, half:T])
+        nc.sync.dma_start(offsets[:], offs)
+        for h in range(PAIRS):
+            for o in range(O):
+                tabs[o, h] = keep.tile([P, 2 * T], BF16, name=f"tab{o}_{h}")
+                if (o, h) != (0, 0):
+                    raws[o, h] = keep.tile([P, 2, T], F32, name=f"raw{o}_{h}")
+                    nc.sync.dma_start(out=raws[o, h][:], in_=raw_view(o, h))
+        norm_t = keep.tile([P, G], F32, name="norm_t")
+        nc.sync.dma_start(out=norm_t[:], in_=norm)
+        w_raw = keep.tile([P, PACK, M], F32, name="w_raw")
+        nc.sync.dma_start(out=w_raw[:], in_=w.rearrange("(p t) m -> p t m", t=PACK))
+        bias_t = [keep.tile([P, 1], F32, name=f"bias{i}") for i in range(2)]
+        for i in range(2):
+            nc.sync.dma_start(out=bias_t[i][:], in_=bias[i * P : (i + 1) * P, :])
+
+        t00 = tabs[0, 0][:].rearrange("p (c t) -> p c t", t=2)
+        nc.scalar.activation(t00[:, 0:half, :], first[0][:].rearrange("p t c -> p c t"), COPY)
+        nc.vector.tensor_copy(t00[:, half:T, :], first[1][:].rearrange("p t c -> p c t"))
+        for h in range(PAIRS):
+            for o in range(O):
+                if (o, h) != (0, 0):
+                    nc.scalar.activation(
+                        tabs[o, h][:].rearrange("p (c t) -> p c t", t=2), raws[o, h][:].rearrange("p t c -> p c t"), COPY
+                    )
+        w_bf = keep.tile([P, M * PACK], BF16, name="w_bf", align_bytes=64)
+        nc.scalar.activation(w_bf[:].rearrange("p (m t) -> p m t", t=PACK), w_raw[:].rearrange("p t m -> p m t"), COPY)
+        w_codes = keep.tile([P, M], U32, name="w_codes", align_bytes=64)
+        w_scales = keep.tile([P, M], U8, name="w_scales", align_bytes=64)
+
+        gathered = {}
+        sums = {}
+        totals = [keep.tile([P, PAIRS, CHUNK * 2], F32, name=f"total{c}") for c in range(CHUNKS)]
+
+        def gather(h, o, c):
+            gathered[h, o, c] = keep.tile([P, CHUNK], U32, name=f"g{h}_{o}_{c}")
+            col = (o * G + c * CHUNK) // 16
+            nc.vector.tensor_copy(gathered[h, o, c][:], tabs[o, h][:].bitcast(U32).indirect(offsets[:, col : col + CHUNK // 16]))
+
+        def add_two(engine, h, q, c):
+            sums[h, q, c] = keep.tile([P, CHUNK * 2], F32, name=f"s{h}_{q}_{c}")
+            engine.tensor_tensor(
+                sums[h, q, c][:], gathered[h, 2 * q, c][:].bitcast(BF16), gathered[h, 2 * q + 1, c][:].bitcast(BF16), ADD
+            )
+
+        def total(h, c):
+            nc.vector.tensor_tensor(totals[c][:, h, :], sums[h, 0, c][:], sums[h, 1, c][:], ADD)
+
+        scaled = {}
+        codes = {}
+        scales = {}
+
+        def scale(c):
+            scaled[c] = keep.tile([P, CHUNK * PACK], BF16, name=f"e{c}", align_bytes=64)
+            nc.vector.tensor_tensor(
+                scaled[c][:].rearrange("p (g h t) -> p g h t", h=2, t=2),
+                totals[c][:].rearrange("p h (g t) -> p g h t", t=2),
+                norm_t[:, c * CHUNK : (c + 1) * CHUNK].unsqueeze(2).unsqueeze(3).to_broadcast([P, CHUNK, 2, 2]),
+                MULT,
+            )
+
+        def quantize(c):
+            codes[c] = keep.tile([P, CHUNK], U32, name=f"codes{c}", align_bytes=64)
+            scales[c] = keep.tile([P, CHUNK], U8, name=f"scales{c}", align_bytes=64)
+            nc.vector.quantize_mx(out=codes[c][:].bitcast(FP8X4), scales=scales[c][:], in_=scaled[c][:])
+
+        def product(c):
+            acc = psum.tile([P, 2, CHUNK], F32, name=f"acc{c}")
+            result = keep.tile([P, 2, CHUNK], F32, name=f"result{c}")
+            for i in range(2):
+                nc.tensor.matmul_mx(
+                    out=acc[:, i, :],
+                    lhsT=w_codes[:, i * P : (i + 1) * P].bitcast(FP8X4),
+                    lhsT_scale=w_scales[:, i * P : (i + 1) * P],
+                    rhs=codes[c][:].bitcast(FP8X4),
+                    rhs_scale=scales[c][:],
+                    start=True,
+                    stop=True,
+                )
+            for i in range(2):
+                nc.scalar.activation(result[:, i, :], acc[:, i, :], IDENTITY, bias=bias_t[i][:])
+            nc.sync.dma_start(
+                out=out.rearrange("(i p) g -> p i g", p=P)[:, :, c * CHUNK : (c + 1) * CHUNK], in_=result[:]
+            )
+
+        last = CHUNKS - 1
+
+        def pair_engine(c):
+            return nc.vector if c == last else nc.gpsimd
+
+        for o in range(O):
+            for c in range(CHUNKS):
+                gather(0, o, c)
+                if o % 2 == 1:
+                    add_two(pair_engine(c), 0, o // 2, c)
+        nc.vector.quantize_mx(out=w_codes[:].bitcast(FP8X4), scales=w_scales[:], in_=w_bf[:])
+        for c in range(CHUNKS):
+            for o in range(O):
+                gather(1, o, c)
+                if o % 2 == 1:
+                    add_two(pair_engine(c), 1, o // 2, c)
+            total(0, c)
+            if c > 0:
+                total(1, c - 1)
+                scale(c - 1)
+            if c > 1:
+                quantize(c - 2)
+                product(c - 2)
+        total(1, last)
+        quantize(last - 1)
+        product(last - 1)
+        scale(last)
+        quantize(last)
+        product(last)

@@ -1,13 +1,13 @@
 from contextlib import ExitStack
 
 import concourse.mybir as mybir
+from concourse.masks import make_identity
 
 O, G, T, D, M = 4, 1024, 512, 512, 256
 P = 128
 PACK = 4
 PAIRS = 2
-CHUNK = 256
-CHUNKS = G // CHUNK
+PIECES = ((0, 384), (384, 384), (768, 256))
 FLOPS = 2 * D * M * G
 
 F32 = mybir.dt.float32
@@ -21,19 +21,28 @@ MULT = mybir.AluOpType.mult
 COPY = mybir.ActivationFunctionType.Copy
 IDENTITY = mybir.ActivationFunctionType.Identity
 
+POST = ((0, 256, True), (256, 256, True), (512, 256, True), (768, 128, False), (896, 128, False))
+
 
 def tile_attend_aq_bias_kernel(tc, cb, w, norm, bias, offs, out):
     nc = tc.nc
     with ExitStack() as ctx:
         lists = ctx.enter_context(tc.tile_pool(name="lists", bufs=1))
         keep = ctx.enter_context(tc.tile_pool(name="keep", bufs=1))
-        psum = ctx.enter_context(tc.psum_pool(name="psum", bufs=1))
+        psum_t = ctx.enter_context(tc.psum_pool(name="psum_t", bufs=3))
+        psum_b = ctx.enter_context(tc.psum_pool(name="psum_b", bufs=3))
+        psum_a = ctx.enter_context(tc.psum_pool(name="psum_a", bufs=2))
 
         def raw_view(o, h):
             return cb[o].rearrange("(p t) c -> p t c", t=PACK)[:, 2 * h : 2 * h + 2, :]
 
         raws = {}
-        tabs = {}
+        tables = keep.tile([P, PAIRS * O * T * 2], BF16, name="tables")
+
+        def table(o, h):
+            slot = (1 - h) * O + o
+            return tables[:, slot * 2 * T : (slot + 1) * 2 * T]
+
         half = T // 2
         offsets = lists.tile([P, O * G // 16], U16, name="offsets")
         first = [keep.tile([P, 2, half], F32, name=f"raw_first{i}") for i in range(2)]
@@ -42,7 +51,6 @@ def tile_attend_aq_bias_kernel(tc, cb, w, norm, bias, offs, out):
         nc.sync.dma_start(offsets[:], offs)
         for h in range(PAIRS):
             for o in range(O):
-                tabs[o, h] = keep.tile([P, 2 * T], BF16, name=f"tab{o}_{h}")
                 if (o, h) != (0, 0):
                     raws[o, h] = keep.tile([P, 2, T], F32, name=f"raw{o}_{h}")
                     nc.sync.dma_start(out=raws[o, h][:], in_=raw_view(o, h))
@@ -54,101 +62,178 @@ def tile_attend_aq_bias_kernel(tc, cb, w, norm, bias, offs, out):
         for i in range(2):
             nc.sync.dma_start(out=bias_t[i][:], in_=bias[i * P : (i + 1) * P, :])
 
-        t00 = tabs[0, 0][:].rearrange("p (c t) -> p c t", t=2)
+        ident_f = keep.tile([P, P], F32, name="ident_f")
+        make_identity(nc, ident_f[:])
+        ident_b = keep.tile([P, P], BF16, name="ident_b")
+        make_identity(nc, ident_b[:])
+
+        t00 = table(0, 0).rearrange("p (c t) -> p c t", t=2)
         nc.scalar.activation(t00[:, 0:half, :], first[0][:].rearrange("p t c -> p c t"), COPY)
         nc.vector.tensor_copy(t00[:, half:T, :], first[1][:].rearrange("p t c -> p c t"))
         for h in range(PAIRS):
             for o in range(O):
                 if (o, h) != (0, 0):
                     nc.scalar.activation(
-                        tabs[o, h][:].rearrange("p (c t) -> p c t", t=2), raws[o, h][:].rearrange("p t c -> p c t"), COPY
+                        table(o, h).rearrange("p (c t) -> p c t", t=2), raws[o, h][:].rearrange("p t c -> p c t"), COPY
                     )
-        w_bf = keep.tile([P, M * PACK], BF16, name="w_bf", align_bytes=64)
-        nc.scalar.activation(w_bf[:].rearrange("p (m t) -> p m t", t=PACK), w_raw[:].rearrange("p t m -> p m t"), COPY)
-        w_codes = keep.tile([P, M], U32, name="w_codes", align_bytes=64)
-        w_scales = keep.tile([P, M], U8, name="w_scales", align_bytes=64)
 
         gathered = {}
+        for h in range(PAIRS):
+            for o in range(O):
+                gathered[h, o] = keep.tile([P, G], U32, name=f"g{h}_{o}")
+                slot = (1 - h) * O + o
+                window = tables[:, slot * 2 * T : (slot + (1, 4)[h]) * 2 * T].bitcast(U32)
+                for start, width in (PIECES, ((0, G),))[h]:
+                    col = (o * G + start) // 16
+                    nc.vector.tensor_copy(
+                        gathered[h, o][:, start : start + width],
+                        window.indirect(offsets[:, col : col + width // 16]),
+                    )
+
         sums = {}
-        totals = [keep.tile([P, PAIRS, CHUNK * 2], F32, name=f"total{c}") for c in range(CHUNKS)]
+        for h in range(PAIRS):
+            for q in range(2):
+                sums[h, q] = keep.tile([P, G * 2], F32, name=f"sum{h}_{q}")
 
-        def gather(h, o, c):
-            gathered[h, o, c] = keep.tile([P, CHUNK], U32, name=f"g{h}_{o}_{c}")
-            col = (o * G + c * CHUNK) // 16
-            nc.vector.tensor_copy(gathered[h, o, c][:], tabs[o, h][:].bitcast(U32).indirect(offsets[:, col : col + CHUNK // 16]))
-
-        def add_two(engine, h, q, c):
-            sums[h, q, c] = keep.tile([P, CHUNK * 2], F32, name=f"s{h}_{q}_{c}")
+        def add_two(engine, h, q, start, width):
+            cols = slice(2 * start, 2 * (start + width))
             engine.tensor_tensor(
-                sums[h, q, c][:], gathered[h, 2 * q, c][:].bitcast(BF16), gathered[h, 2 * q + 1, c][:].bitcast(BF16), ADD
+                sums[h, q][:, cols],
+                gathered[h, 2 * q][:].bitcast(BF16)[:, cols],
+                gathered[h, 2 * q + 1][:].bitcast(BF16)[:, cols],
+                ADD,
             )
 
-        def total(h, c):
-            nc.vector.tensor_tensor(totals[c][:, h, :], sums[h, 0, c][:], sums[h, 1, c][:], ADD)
+        totals = {}
+        for i, (start, width, turned) in enumerate(POST):
+            totals[i] = keep.tile([P, PACK, width], F32, name=f"total{i}")
+
+        def total(engine, h, i):
+            start, width, turned = POST[i]
+            cols = slice(2 * start, 2 * (start + width))
+            engine.tensor_tensor(
+                totals[i][:, 2 * h : 2 * h + 2, :],
+                sums[h, 0][:, cols].rearrange("p (g t) -> p t g", t=2),
+                sums[h, 1][:, cols].rearrange("p (g t) -> p t g", t=2),
+                ADD,
+            )
+
+        norm_cols = keep.tile([P, G // P], F32, name="norm_cols")
+        for half_i in range(2):
+            turned_norm = psum_t.tile([P, 4, P], F32, name="turn")
+            for b in range(4):
+                block = half_i * 4 + b
+                nc.tensor.transpose(turned_norm[:, b, :], norm_t[:, block * P : (block + 1) * P], ident_f[:])
+            nc.scalar.copy(norm_cols[:, half_i * 4 : half_i * 4 + 4], turned_norm[:, :, 0])
+
+        backs = {}
+        for i, (start, width, turned) in enumerate(POST):
+            if turned:
+                backs[i] = psum_b.tile([P, PACK, width], BF16, name="back")
+
+        def scale_by_turning(h, i):
+            start, width, turned = POST[i]
+            blocks = width // P
+            turn = psum_t.tile([P, blocks, 2, P], F32, name="turn")
+            for b in range(blocks):
+                for t in range(2):
+                    nc.tensor.transpose(turn[:, b, t, :], totals[i][:, 2 * h + t, b * P : (b + 1) * P], ident_f[:])
+            scaled_t = keep.tile([P, blocks, 2, P], BF16, name=f"scaled_t{h}_{i}")
+            for b in range(blocks):
+                block = start // P + b
+                nc.scalar.activation(scaled_t[:, b, :, :], turn[:, b, :, :], COPY, scale=norm_cols[:, block : block + 1])
+            for b in range(blocks):
+                for t in range(2):
+                    nc.tensor.transpose(backs[i][:, 2 * h + t, b * P : (b + 1) * P], scaled_t[:, b, t, :], ident_b[:])
 
         scaled = {}
         codes = {}
         scales = {}
+        for i, (start, width, turned) in enumerate(POST):
+            scaled[i] = keep.tile([P, width * PACK], BF16, name=f"e{i}", align_bytes=64)
+            codes[i] = keep.tile([P, width], U32, name=f"codes{i}", align_bytes=64)
+            scales[i] = keep.tile([P, width], U8, name=f"scales{i}", align_bytes=64)
 
-        def scale(c):
-            scaled[c] = keep.tile([P, CHUNK * PACK], BF16, name=f"e{c}", align_bytes=64)
+        def interleave(i):
+            nc.scalar.copy(scaled[i][:].rearrange("p (g t) -> p g t", t=PACK), backs[i][:].rearrange("p t g -> p g t"))
+
+        def scale_in_place(i):
+            start, width, turned = POST[i]
             nc.vector.tensor_tensor(
-                scaled[c][:].rearrange("p (g h t) -> p g h t", h=2, t=2),
-                totals[c][:].rearrange("p h (g t) -> p g h t", t=2),
-                norm_t[:, c * CHUNK : (c + 1) * CHUNK].unsqueeze(2).unsqueeze(3).to_broadcast([P, CHUNK, 2, 2]),
+                scaled[i][:].rearrange("p (g t) -> p g t", t=PACK),
+                totals[i][:].rearrange("p t g -> p g t"),
+                norm_t[:, start : start + width].unsqueeze(2).to_broadcast([P, width, PACK]),
                 MULT,
             )
 
-        def quantize(c):
-            codes[c] = keep.tile([P, CHUNK], U32, name=f"codes{c}", align_bytes=64)
-            scales[c] = keep.tile([P, CHUNK], U8, name=f"scales{c}", align_bytes=64)
-            nc.vector.quantize_mx(out=codes[c][:].bitcast(FP8X4), scales=scales[c][:], in_=scaled[c][:])
+        def quantize(i):
+            nc.vector.quantize_mx(out=codes[i][:].bitcast(FP8X4), scales=scales[i][:], in_=scaled[i][:])
 
-        def product(c):
-            acc = psum.tile([P, 2, CHUNK], F32, name=f"acc{c}")
-            result = keep.tile([P, 2, CHUNK], F32, name=f"result{c}")
-            for i in range(2):
+        w_bf = keep.tile([P, M * PACK], BF16, name="w_bf", align_bytes=64)
+        w_codes = keep.tile([P, M], U32, name="w_codes", align_bytes=64)
+        w_scales = keep.tile([P, M], U8, name="w_scales", align_bytes=64)
+
+        def product(i):
+            start, width, turned = POST[i]
+            acc = psum_a.tile([P, 2, width], F32, name="acc")
+            result = keep.tile([P, 2, width], F32, name=f"result{i}")
+            for j in range(2):
                 nc.tensor.matmul_mx(
-                    out=acc[:, i, :],
-                    lhsT=w_codes[:, i * P : (i + 1) * P].bitcast(FP8X4),
-                    lhsT_scale=w_scales[:, i * P : (i + 1) * P],
-                    rhs=codes[c][:].bitcast(FP8X4),
-                    rhs_scale=scales[c][:],
+                    out=acc[:, j, :],
+                    lhsT=w_codes[:, j * P : (j + 1) * P].bitcast(FP8X4),
+                    lhsT_scale=w_scales[:, j * P : (j + 1) * P],
+                    rhs=codes[i][:].bitcast(FP8X4),
+                    rhs_scale=scales[i][:],
                     start=True,
                     stop=True,
                 )
-            for i in range(2):
-                nc.scalar.activation(result[:, i, :], acc[:, i, :], IDENTITY, bias=bias_t[i][:])
-            nc.sync.dma_start(
-                out=out.rearrange("(i p) g -> p i g", p=P)[:, :, c * CHUNK : (c + 1) * CHUNK], in_=result[:]
-            )
+            for j in range(2):
+                nc.scalar.activation(result[:, j, :], acc[:, j, :], IDENTITY, bias=bias_t[j][:])
+            nc.sync.dma_start(out=out.rearrange("(j p) g -> p j g", p=P)[:, :, start : start + width], in_=result[:])
 
-        last = CHUNKS - 1
-
-        def pair_engine(c):
-            return nc.vector if c == last else nc.gpsimd
-
-        for o in range(O):
-            for c in range(CHUNKS):
-                gather(0, o, c)
-                if o % 2 == 1:
-                    add_two(pair_engine(c), 0, o // 2, c)
+        for q in range(2):
+            for start, width in PIECES:
+                add_two(nc.gpsimd, 0, q, start, width)
+        nc.scalar.activation(w_bf[:].rearrange("p (m t) -> p m t", t=PACK), w_raw[:].rearrange("p t m -> p m t"), COPY)
         nc.vector.quantize_mx(out=w_codes[:].bitcast(FP8X4), scales=w_scales[:], in_=w_bf[:])
-        for c in range(CHUNKS):
-            for o in range(O):
-                gather(1, o, c)
-                if o % 2 == 1:
-                    add_two(pair_engine(c), 1, o // 2, c)
-            total(0, c)
-            if c > 0:
-                total(1, c - 1)
-                scale(c - 1)
-            if c > 1:
-                quantize(c - 2)
-                product(c - 2)
-        total(1, last)
-        quantize(last - 1)
-        product(last - 1)
-        scale(last)
-        quantize(last)
-        product(last)
+        n = len(POST)
+        for i in range(n):
+            total(nc.gpsimd, 0, i)
+            if POST[i][2]:
+                scale_by_turning(0, i)
+        def post_add(q, i):
+            add_two(nc.vector, 1, q, POST[i][0], POST[i][1])
+
+        def finish_total(i):
+            total(nc.vector, 1, i)
+            if POST[i][2]:
+                scale_by_turning(1, i)
+                interleave(i)
+
+        add_two(nc.gpsimd, 1, 0, POST[0][0], POST[0][1])
+        post_add(1, 0)
+        post_add(0, 1)
+        finish_total(0)
+        post_add(1, 1)
+        post_add(0, 2)
+        finish_total(1)
+        post_add(1, 2)
+        post_add(0, 3)
+        finish_total(2)
+        post_add(1, 3)
+        post_add(0, 4)
+        finish_total(3)
+        quantize(0)
+        product(0)
+        post_add(1, 4)
+        scale_in_place(3)
+        finish_total(4)
+        quantize(1)
+        product(1)
+        scale_in_place(4)
+        quantize(3)
+        product(3)
+        quantize(2)
+        product(2)
+        quantize(4)
+        product(4)

@@ -7,7 +7,8 @@ O, G, T, D, M = 4, 1024, 512, 512, 256
 P = 128
 PACK = 4
 PAIRS = 2
-PIECES = ((0, 384), (384, 384), (768, 256))
+THIRDS = ((0, 384), (384, 384), (768, 256))
+HALVES = ((0, 512), (512, 512))
 FLOPS = 2 * D * M * G
 
 F32 = mybir.dt.float32
@@ -22,6 +23,7 @@ COPY = mybir.ActivationFunctionType.Copy
 IDENTITY = mybir.ActivationFunctionType.Identity
 
 POST = ((0, 256, True), (256, 256, True), (512, 256, True), (768, 128, False), (896, 128, False))
+GPSIMD_TOTALS = (0, 1)
 
 
 def tile_attend_aq_bias_kernel(tc, cb, w, norm, bias, offs, out):
@@ -29,9 +31,8 @@ def tile_attend_aq_bias_kernel(tc, cb, w, norm, bias, offs, out):
     with ExitStack() as ctx:
         lists = ctx.enter_context(tc.tile_pool(name="lists", bufs=1))
         keep = ctx.enter_context(tc.tile_pool(name="keep", bufs=1))
-        psum_t = ctx.enter_context(tc.psum_pool(name="psum_t", bufs=3))
+        psum_t = ctx.enter_context(tc.psum_pool(name="psum_t", bufs=5))
         psum_b = ctx.enter_context(tc.psum_pool(name="psum_b", bufs=3))
-        psum_a = ctx.enter_context(tc.psum_pool(name="psum_a", bufs=2))
 
         def raw_view(o, h):
             return cb[o].rearrange("(p t) c -> p t c", t=PACK)[:, 2 * h : 2 * h + 2, :]
@@ -40,7 +41,7 @@ def tile_attend_aq_bias_kernel(tc, cb, w, norm, bias, offs, out):
         tables = keep.tile([P, PAIRS * O * T * 2], BF16, name="tables")
 
         def table(o, h):
-            slot = (1 - h) * O + o
+            slot = PAIRS * O - 1 - (h * O + o)
             return tables[:, slot * 2 * T : (slot + 1) * 2 * T]
 
         half = T // 2
@@ -81,14 +82,22 @@ def tile_attend_aq_bias_kernel(tc, cb, w, norm, bias, offs, out):
         for h in range(PAIRS):
             for o in range(O):
                 gathered[h, o] = keep.tile([P, G], U32, name=f"g{h}_{o}")
-                slot = (1 - h) * O + o
-                window = tables[:, slot * 2 * T : (slot + (1, 4)[h]) * 2 * T].bitcast(U32)
-                for start, width in (PIECES, ((0, G),))[h]:
-                    col = (o * G + start) // 16
-                    nc.vector.tensor_copy(
-                        gathered[h, o][:, start : start + width],
-                        window.indirect(offsets[:, col : col + width // 16]),
-                    )
+
+        def gather(h, o, start, width, slots):
+            slot = PAIRS * O - 1 - (h * O + o)
+            window = tables[:, slot * 2 * T : (slot + slots) * 2 * T].bitcast(U32)
+            col = (o * G + start) // 16
+            nc.vector.tensor_copy(
+                gathered[h, o][:, start : start + width], window.indirect(offsets[:, col : col + width // 16])
+            )
+
+        for o, j in ((0, 0), (0, 1), (1, 0), (0, 2), (1, 1), (1, 2)):
+            gather(0, o, *THIRDS[j], 1)
+        gather(0, 2, 0, G, 3)
+        for start, width in HALVES:
+            gather(0, 3, start, width, 4)
+        for o in range(O):
+            gather(1, o, 0, G, 4)
 
         sums = {}
         for h in range(PAIRS):
@@ -106,15 +115,15 @@ def tile_attend_aq_bias_kernel(tc, cb, w, norm, bias, offs, out):
 
         totals = {}
         for i, (start, width, turned) in enumerate(POST):
-            totals[i] = keep.tile([P, PACK, width], F32, name=f"total{i}")
+            totals[i] = keep.tile([P, PAIRS, 2 * width], F32, name=f"total{i}")
 
         def total(engine, h, i):
             start, width, turned = POST[i]
             cols = slice(2 * start, 2 * (start + width))
             engine.tensor_tensor(
-                totals[i][:, 2 * h : 2 * h + 2, :],
-                sums[h, 0][:, cols].rearrange("p (g t) -> p t g", t=2),
-                sums[h, 1][:, cols].rearrange("p (g t) -> p t g", t=2),
+                totals[i][:, h, :],
+                sums[h, 0][:, cols],
+                sums[h, 1][:, cols],
                 ADD,
             )
 
@@ -137,7 +146,7 @@ def tile_attend_aq_bias_kernel(tc, cb, w, norm, bias, offs, out):
             turn = psum_t.tile([P, blocks, 2, P], F32, name="turn")
             for b in range(blocks):
                 for t in range(2):
-                    nc.tensor.transpose(turn[:, b, t, :], totals[i][:, 2 * h + t, b * P : (b + 1) * P], ident_f[:])
+                    nc.tensor.transpose(turn[:, b, t, :], totals[i][:, h, 2 * b * P + t : 2 * (b + 1) * P : 2], ident_f[:])
             scaled_t = keep.tile([P, blocks, 2, P], BF16, name=f"scaled_t{h}_{i}")
             for b in range(blocks):
                 block = start // P + b
@@ -160,9 +169,9 @@ def tile_attend_aq_bias_kernel(tc, cb, w, norm, bias, offs, out):
         def scale_in_place(i):
             start, width, turned = POST[i]
             nc.vector.tensor_tensor(
-                scaled[i][:].rearrange("p (g t) -> p g t", t=PACK),
-                totals[i][:].rearrange("p t g -> p g t"),
-                norm_t[:, start : start + width].unsqueeze(2).to_broadcast([P, width, PACK]),
+                scaled[i][:].rearrange("p (g h t) -> p g h t", h=PAIRS, t=2),
+                totals[i][:].rearrange("p h (g t) -> p g h t", t=2),
+                norm_t[:, start : start + width].unsqueeze(2).unsqueeze(3).to_broadcast([P, width, PAIRS, 2]),
                 MULT,
             )
 
@@ -175,11 +184,18 @@ def tile_attend_aq_bias_kernel(tc, cb, w, norm, bias, offs, out):
 
         def product(i):
             start, width, turned = POST[i]
-            acc = psum_a.tile([P, 2, width], F32, name="acc")
+            if i < n - 1:
+                both = psum_t.tile([P, 2, width], F32, name="turn")
+                acc = [both[:, j, :] for j in range(2)]
+            else:
+                acc = []
+                for j in range(2):
+                    one = psum_t.tile([P, width], F32, name="turn")
+                    acc.append(one[:])
             result = keep.tile([P, 2, width], F32, name=f"result{i}")
             for j in range(2):
                 nc.tensor.matmul_mx(
-                    out=acc[:, j, :],
+                    out=acc[j],
                     lhsT=w_codes[:, j * P : (j + 1) * P].bitcast(FP8X4),
                     lhsT_scale=w_scales[:, j * P : (j + 1) * P],
                     rhs=codes[i][:].bitcast(FP8X4),
@@ -187,22 +203,20 @@ def tile_attend_aq_bias_kernel(tc, cb, w, norm, bias, offs, out):
                     start=True,
                     stop=True,
                 )
-            for j in range(2):
-                nc.scalar.activation(result[:, j, :], acc[:, j, :], IDENTITY, bias=bias_t[j][:])
-            nc.sync.dma_start(out=out.rearrange("(j p) g -> p j g", p=P)[:, :, start : start + width], in_=result[:])
+            out_cols = out.rearrange("(j p) g -> p j g", p=P)[:, :, start : start + width]
+            nc.scalar.activation(result[:, 0, :], acc[0], IDENTITY, bias=bias_t[0][:])
+            if i < n - 1:
+                nc.scalar.activation(result[:, 1, :], acc[1], IDENTITY, bias=bias_t[1][:])
+                nc.sync.dma_start(out=out_cols, in_=result[:])
+            else:
+                nc.vector.tensor_scalar(out=result[:, 1, :], in0=acc[1], scalar1=bias_t[1][:], scalar2=None, op0=ADD)
+                for j in range(2):
+                    nc.sync.dma_start(out=out_cols[:, j, :], in_=result[:, j, :])
 
-        for q in range(2):
-            for start, width in PIECES:
-                add_two(nc.gpsimd, 0, q, start, width)
-        nc.scalar.activation(w_bf[:].rearrange("p (m t) -> p m t", t=PACK), w_raw[:].rearrange("p t m -> p m t"), COPY)
-        nc.vector.quantize_mx(out=w_codes[:].bitcast(FP8X4), scales=w_scales[:], in_=w_bf[:])
         n = len(POST)
-        for i in range(n):
-            total(nc.gpsimd, 0, i)
-            if POST[i][2]:
-                scale_by_turning(0, i)
-        def post_add(q, i):
-            add_two(nc.vector, 1, q, POST[i][0], POST[i][1])
+        for q, pieces in enumerate((THIRDS, HALVES)):
+            for start, width in pieces:
+                add_two(nc.gpsimd, 0, q, start, width)
 
         def finish_total(i):
             total(nc.vector, 1, i)
@@ -210,30 +224,40 @@ def tile_attend_aq_bias_kernel(tc, cb, w, norm, bias, offs, out):
                 scale_by_turning(1, i)
                 interleave(i)
 
-        add_two(nc.gpsimd, 1, 0, POST[0][0], POST[0][1])
-        post_add(1, 0)
-        post_add(0, 1)
+        def finish(i):
+            quantize(i)
+            product(i)
+
+        def post_adds(i):
+            add_two(nc.vector, 1, 0, POST[i][0], POST[i][1])
+            add_two(nc.vector, 1, 1, POST[i][0], POST[i][1])
+
+        def first_total(i):
+            total(nc.gpsimd if i in GPSIMD_TOTALS else nc.vector, 0, i)
+            if POST[i][2]:
+                scale_by_turning(0, i)
+
+        first_total(0)
+        post_adds(0)
+        first_total(1)
         finish_total(0)
-        post_add(1, 1)
-        post_add(0, 2)
+        post_adds(1)
+        first_total(2)
         finish_total(1)
-        post_add(1, 2)
-        post_add(0, 3)
+        post_adds(2)
+        first_total(3)
         finish_total(2)
-        post_add(1, 3)
-        post_add(0, 4)
+        post_adds(3)
+        first_total(4)
         finish_total(3)
-        quantize(0)
-        product(0)
-        post_add(1, 4)
+        post_adds(4)
+        nc.scalar.activation(w_bf[:].rearrange("p (m t) -> p m t", t=PACK), w_raw[:].rearrange("p t m -> p m t"), COPY)
+        nc.vector.quantize_mx(out=w_codes[:].bitcast(FP8X4), scales=w_scales[:], in_=w_bf[:])
         scale_in_place(3)
+        finish(0)
         finish_total(4)
-        quantize(1)
-        product(1)
+        finish(1)
+        finish(3)
         scale_in_place(4)
-        quantize(3)
-        product(3)
-        quantize(2)
-        product(2)
-        quantize(4)
-        product(4)
+        finish(2)
+        finish(4)

@@ -7,8 +7,7 @@ O, G, T, D, M = 4, 1024, 512, 512, 256
 P = 128
 PACK = 4
 PAIRS = 2
-THIRDS = ((0, 384), (384, 384), (768, 256))
-HALVES = ((0, 512), (512, 512))
+M_TILES = M // P
 FLOPS = 2 * D * M * G
 
 F32 = mybir.dt.float32
@@ -22,242 +21,208 @@ MULT = mybir.AluOpType.mult
 COPY = mybir.ActivationFunctionType.Copy
 IDENTITY = mybir.ActivationFunctionType.Identity
 
-POST = ((0, 256, True), (256, 256, True), (512, 256, True), (768, 128, False), (896, 128, False))
-GPSIMD_TOTALS = (0, 1)
+THIRDS = ((0, 384), (384, 384), (768, 256))
+HALVES = ((0, 512), (512, 512))
+TURNED = ((0, 256), (256, 256))
+DIRECT = ((512, 256), (768, 128), (896, 128))
 
 
 def tile_attend_aq_bias_kernel(tc, cb, w, norm, bias, offs, out):
     nc = tc.nc
     with ExitStack() as ctx:
-        lists = ctx.enter_context(tc.tile_pool(name="lists", bufs=1))
         keep = ctx.enter_context(tc.tile_pool(name="keep", bufs=1))
-        psum_t = ctx.enter_context(tc.psum_pool(name="psum_t", bufs=5))
-        psum_b = ctx.enter_context(tc.psum_pool(name="psum_b", bufs=3))
+        psum = ctx.enter_context(tc.psum_pool(name="psum", bufs=6))
+        psum_back = ctx.enter_context(tc.psum_pool(name="psum_back", bufs=2))
 
-        def raw_view(o, h):
+        def pair_rows(o, h):
             return cb[o].rearrange("(p t) c -> p t c", t=PACK)[:, 2 * h : 2 * h + 2, :]
 
-        raws = {}
+        offsets = keep.tile([P, O * G // 16], U16, name="offsets")
         tables = keep.tile([P, PAIRS * O * T * 2], BF16, name="tables")
 
-        def table(o, h):
+        def table_at(o, h, slots):
             slot = PAIRS * O - 1 - (h * O + o)
-            return tables[:, slot * 2 * T : (slot + 1) * 2 * T]
+            return tables[:, slot * 2 * T : (slot + slots) * 2 * T]
 
         half = T // 2
-        offsets = lists.tile([P, O * G // 16], U16, name="offsets")
-        first = [keep.tile([P, 2, half], F32, name=f"raw_first{i}") for i in range(2)]
-        nc.sync.dma_start(out=first[0][:], in_=raw_view(0, 0)[:, :, 0:half])
-        nc.sync.dma_start(out=first[1][:], in_=raw_view(0, 0)[:, :, half:T])
+        raw_halves = [keep.tile([P, 2, half], F32, name=f"raw_half{i}") for i in range(2)]
+        for i in range(2):
+            nc.sync.dma_start(out=raw_halves[i][:], in_=pair_rows(0, 0)[:, :, i * half : (i + 1) * half])
         nc.sync.dma_start(offsets[:], offs)
-        for h in range(PAIRS):
-            for o in range(O):
-                if (o, h) != (0, 0):
-                    raws[o, h] = keep.tile([P, 2, T], F32, name=f"raw{o}_{h}")
-                    nc.sync.dma_start(out=raws[o, h][:], in_=raw_view(o, h))
-        norm_t = keep.tile([P, G], F32, name="norm_t")
-        nc.sync.dma_start(out=norm_t[:], in_=norm)
+        order = [(h, o) for h in range(PAIRS) for o in range(O)]
+        raws = {}
+        for h, o in order[1:]:
+            raws[h, o] = keep.tile([P, 2, T], F32, name=f"raw{h}_{o}")
+            nc.sync.dma_start(out=raws[h, o][:], in_=pair_rows(o, h))
+        norm_rows = keep.tile([P, G], F32, name="norm_rows")
+        nc.sync.dma_start(out=norm_rows[:], in_=norm)
         w_raw = keep.tile([P, PACK, M], F32, name="w_raw")
         nc.sync.dma_start(out=w_raw[:], in_=w.rearrange("(p t) m -> p t m", t=PACK))
-        bias_t = [keep.tile([P, 1], F32, name=f"bias{i}") for i in range(2)]
-        for i in range(2):
-            nc.sync.dma_start(out=bias_t[i][:], in_=bias[i * P : (i + 1) * P, :])
+        bias_cols = [keep.tile([P, 1], F32, name=f"bias{j}") for j in range(M_TILES)]
+        for j in range(M_TILES):
+            nc.sync.dma_start(out=bias_cols[j][:], in_=bias[j * P : (j + 1) * P, :])
 
-        ident_f = keep.tile([P, P], F32, name="ident_f")
-        make_identity(nc, ident_f[:])
-        ident_b = keep.tile([P, P], BF16, name="ident_b")
-        make_identity(nc, ident_b[:])
+        ident_f32 = keep.tile([P, P], F32, name="ident_f32")
+        make_identity(nc, ident_f32[:])
+        ident_bf16 = keep.tile([P, P], BF16, name="ident_bf16")
+        make_identity(nc, ident_bf16[:])
 
-        t00 = table(0, 0).rearrange("p (c t) -> p c t", t=2)
-        nc.scalar.activation(t00[:, 0:half, :], first[0][:].rearrange("p t c -> p c t"), COPY)
-        nc.vector.tensor_copy(t00[:, half:T, :], first[1][:].rearrange("p t c -> p c t"))
-        for h in range(PAIRS):
-            for o in range(O):
-                if (o, h) != (0, 0):
-                    nc.scalar.activation(
-                        table(o, h).rearrange("p (c t) -> p c t", t=2), raws[o, h][:].rearrange("p t c -> p c t"), COPY
-                    )
-
-        gathered = {}
-        for h in range(PAIRS):
-            for o in range(O):
-                gathered[h, o] = keep.tile([P, G], U32, name=f"g{h}_{o}")
-
-        def gather(h, o, start, width, slots):
-            slot = PAIRS * O - 1 - (h * O + o)
-            window = tables[:, slot * 2 * T : (slot + slots) * 2 * T].bitcast(U32)
-            col = (o * G + start) // 16
-            nc.vector.tensor_copy(
-                gathered[h, o][:, start : start + width], window.indirect(offsets[:, col : col + width // 16])
+        first = table_at(0, 0, 1).rearrange("p (c t) -> p c t", t=2)
+        nc.scalar.activation(first[:, 0:half, :], raw_halves[0][:].rearrange("p t c -> p c t"), COPY)
+        nc.vector.tensor_copy(first[:, half:T, :], raw_halves[1][:].rearrange("p t c -> p c t"))
+        for h, o in order[1:]:
+            nc.scalar.activation(
+                table_at(o, h, 1).rearrange("p (c t) -> p c t", t=2), raws[h, o][:].rearrange("p t c -> p c t"), COPY
             )
 
-        for o, j in ((0, 0), (0, 1), (1, 0), (0, 2), (1, 1), (1, 2)):
-            gather(0, o, *THIRDS[j], 1)
+        words = {(h, o): keep.tile([P, G], U32, name=f"words{h}_{o}") for h, o in order}
+
+        def gather(h, o, start, width, slots):
+            col = (o * G + start) // 16
+            nc.vector.tensor_copy(
+                words[h, o][:, start : start + width],
+                table_at(o, h, slots).bitcast(U32).indirect(offsets[:, col : col + width // 16]),
+            )
+
+        for o, piece in ((0, 0), (0, 1), (1, 0), (0, 2), (1, 1), (1, 2)):
+            gather(0, o, *THIRDS[piece], 1)
         gather(0, 2, 0, G, 3)
         for start, width in HALVES:
             gather(0, 3, start, width, 4)
         for o in range(O):
             gather(1, o, 0, G, 4)
 
-        sums = {}
-        for h in range(PAIRS):
-            for q in range(2):
-                sums[h, q] = keep.tile([P, G * 2], F32, name=f"sum{h}_{q}")
+        halfsums = {(h, q): keep.tile([P, 2 * G], F32, name=f"halfsum{h}_{q}") for h in range(PAIRS) for q in range(2)}
+        sums = keep.tile([P, PAIRS, 2 * G], F32, name="sums")
 
-        def add_two(engine, h, q, start, width):
+        def add_words(engine, h, q, start, width):
             cols = slice(2 * start, 2 * (start + width))
             engine.tensor_tensor(
-                sums[h, q][:, cols],
-                gathered[h, 2 * q][:].bitcast(BF16)[:, cols],
-                gathered[h, 2 * q + 1][:].bitcast(BF16)[:, cols],
+                halfsums[h, q][:, cols],
+                words[h, 2 * q][:].bitcast(BF16)[:, cols],
+                words[h, 2 * q + 1][:].bitcast(BF16)[:, cols],
                 ADD,
             )
 
-        totals = {}
-        for i, (start, width, turned) in enumerate(POST):
-            totals[i] = keep.tile([P, PAIRS, 2 * width], F32, name=f"total{i}")
-
-        def total(engine, h, i):
-            start, width, turned = POST[i]
+        def add_halfsums(engine, h, start, width):
             cols = slice(2 * start, 2 * (start + width))
-            engine.tensor_tensor(
-                totals[i][:, h, :],
-                sums[h, 0][:, cols],
-                sums[h, 1][:, cols],
-                ADD,
-            )
+            engine.tensor_tensor(sums[:, h, cols], halfsums[h, 0][:, cols], halfsums[h, 1][:, cols], ADD)
 
         norm_cols = keep.tile([P, G // P], F32, name="norm_cols")
-        for half_i in range(2):
-            turned_norm = psum_t.tile([P, 4, P], F32, name="turn")
+        for part in range(2):
+            turned = psum.tile([P, 4, P], F32, name="bank")
             for b in range(4):
-                block = half_i * 4 + b
-                nc.tensor.transpose(turned_norm[:, b, :], norm_t[:, block * P : (block + 1) * P], ident_f[:])
-            nc.scalar.copy(norm_cols[:, half_i * 4 : half_i * 4 + 4], turned_norm[:, :, 0])
+                block = part * 4 + b
+                nc.tensor.transpose(turned[:, b, :], norm_rows[:, block * P : (block + 1) * P], ident_f32[:])
+            nc.scalar.copy(norm_cols[:, part * 4 : part * 4 + 4], turned[:, :, 0])
 
         backs = {}
-        for i, (start, width, turned) in enumerate(POST):
-            if turned:
-                backs[i] = psum_b.tile([P, PACK, width], BF16, name="back")
-
-        def scale_by_turning(h, i):
-            start, width, turned = POST[i]
-            blocks = width // P
-            turn = psum_t.tile([P, blocks, 2, P], F32, name="turn")
-            for b in range(blocks):
-                for t in range(2):
-                    nc.tensor.transpose(turn[:, b, t, :], totals[i][:, h, 2 * b * P + t : 2 * (b + 1) * P : 2], ident_f[:])
-            scaled_t = keep.tile([P, blocks, 2, P], BF16, name=f"scaled_t{h}_{i}")
-            for b in range(blocks):
-                block = start // P + b
-                nc.scalar.activation(scaled_t[:, b, :, :], turn[:, b, :, :], COPY, scale=norm_cols[:, block : block + 1])
-            for b in range(blocks):
-                for t in range(2):
-                    nc.tensor.transpose(backs[i][:, 2 * h + t, b * P : (b + 1) * P], scaled_t[:, b, t, :], ident_b[:])
-
-        scaled = {}
+        grouped = {}
         codes = {}
         scales = {}
-        for i, (start, width, turned) in enumerate(POST):
-            scaled[i] = keep.tile([P, width * PACK], BF16, name=f"e{i}", align_bytes=64)
-            codes[i] = keep.tile([P, width], U32, name=f"codes{i}", align_bytes=64)
-            scales[i] = keep.tile([P, width], U8, name=f"scales{i}", align_bytes=64)
+        for start, width in TURNED + DIRECT:
+            grouped[start] = keep.tile([P, width * PACK], BF16, name=f"grouped{start}", align_bytes=64)
+            codes[start] = keep.tile([P, width], U32, name=f"codes{start}", align_bytes=64)
+            scales[start] = keep.tile([P, width], U8, name=f"scales{start}", align_bytes=64)
+        for start, width in TURNED:
+            backs[start] = psum_back.tile([P, PACK, width], BF16, name="back")
 
-        def interleave(i):
-            nc.scalar.copy(scaled[i][:].rearrange("p (g t) -> p g t", t=PACK), backs[i][:].rearrange("p t g -> p g t"))
+        def scale_turned(h, start, width):
+            blocks = width // P
+            turned = psum.tile([P, blocks, 2, P], F32, name="bank")
+            for b in range(blocks):
+                for t in range(2):
+                    first_col = 2 * (start + b * P) + t
+                    nc.tensor.transpose(turned[:, b, t, :], sums[:, h, first_col : first_col + 2 * P - 1 : 2], ident_f32[:])
+            scaled = keep.tile([P, blocks, 2, P], BF16, name=f"scaled{h}_{start}")
+            for b in range(blocks):
+                block = start // P + b
+                nc.scalar.activation(scaled[:, b, :, :], turned[:, b, :, :], COPY, scale=norm_cols[:, block : block + 1])
+            for b in range(blocks):
+                for t in range(2):
+                    nc.tensor.transpose(backs[start][:, 2 * h + t, b * P : (b + 1) * P], scaled[:, b, t, :], ident_bf16[:])
 
-        def scale_in_place(i):
-            start, width, turned = POST[i]
+        def group_turned(start, width):
+            nc.scalar.copy(
+                grouped[start][:].rearrange("p (g t) -> p g t", t=PACK), backs[start][:].rearrange("p t g -> p g t")
+            )
+
+        def scale_direct(start, width):
             nc.vector.tensor_tensor(
-                scaled[i][:].rearrange("p (g h t) -> p g h t", h=PAIRS, t=2),
-                totals[i][:].rearrange("p h (g t) -> p g h t", t=2),
-                norm_t[:, start : start + width].unsqueeze(2).unsqueeze(3).to_broadcast([P, width, PAIRS, 2]),
+                grouped[start][:].rearrange("p (g h t) -> p g h t", h=PAIRS, t=2),
+                sums[:, :, 2 * start : 2 * (start + width)].rearrange("p h (g t) -> p g h t", t=2),
+                norm_rows[:, start : start + width].unsqueeze(2).unsqueeze(3).to_broadcast([P, width, PAIRS, 2]),
                 MULT,
             )
 
-        def quantize(i):
-            nc.vector.quantize_mx(out=codes[i][:].bitcast(FP8X4), scales=scales[i][:], in_=scaled[i][:])
+        def quantize(start, width):
+            nc.vector.quantize_mx(out=codes[start][:].bitcast(FP8X4), scales=scales[start][:], in_=grouped[start][:])
 
-        w_bf = keep.tile([P, M * PACK], BF16, name="w_bf", align_bytes=64)
+        w_grouped = keep.tile([P, M * PACK], BF16, name="w_grouped", align_bytes=64)
         w_codes = keep.tile([P, M], U32, name="w_codes", align_bytes=64)
         w_scales = keep.tile([P, M], U8, name="w_scales", align_bytes=64)
 
-        def product(i):
-            start, width, turned = POST[i]
-            if i < n - 1:
-                both = psum_t.tile([P, 2, width], F32, name="turn")
-                acc = [both[:, j, :] for j in range(2)]
-            else:
-                acc = []
-                for j in range(2):
-                    one = psum_t.tile([P, width], F32, name="turn")
-                    acc.append(one[:])
-            result = keep.tile([P, 2, width], F32, name=f"result{i}")
-            for j in range(2):
+        def multiply(start, width, on_vector):
+            acc = psum.tile([P, M_TILES, width], F32, name="bank")
+            for j in range(M_TILES):
                 nc.tensor.matmul_mx(
-                    out=acc[j],
+                    out=acc[:, j, :],
                     lhsT=w_codes[:, j * P : (j + 1) * P].bitcast(FP8X4),
                     lhsT_scale=w_scales[:, j * P : (j + 1) * P],
-                    rhs=codes[i][:].bitcast(FP8X4),
-                    rhs_scale=scales[i][:],
+                    rhs=codes[start][:].bitcast(FP8X4),
+                    rhs_scale=scales[start][:],
                     start=True,
                     stop=True,
                 )
-            out_cols = out.rearrange("(j p) g -> p j g", p=P)[:, :, start : start + width]
-            nc.scalar.activation(result[:, 0, :], acc[0], IDENTITY, bias=bias_t[0][:])
-            if i < n - 1:
-                nc.scalar.activation(result[:, 1, :], acc[1], IDENTITY, bias=bias_t[1][:])
-                nc.sync.dma_start(out=out_cols, in_=result[:])
-            else:
-                nc.vector.tensor_scalar(out=result[:, 1, :], in0=acc[1], scalar1=bias_t[1][:], scalar2=None, op0=ADD)
-                for j in range(2):
-                    nc.sync.dma_start(out=out_cols[:, j, :], in_=result[:, j, :])
+            result = keep.tile([P, M_TILES, width], F32, name=f"result{start}")
+            for j in range(M_TILES):
+                if on_vector:
+                    nc.vector.tensor_scalar(
+                        out=result[:, j, :], in0=acc[:, j, :], scalar1=bias_cols[j][:], scalar2=None, op0=ADD
+                    )
+                else:
+                    nc.scalar.activation(result[:, j, :], acc[:, j, :], IDENTITY, bias=bias_cols[j][:])
+            nc.sync.dma_start(
+                out=out.rearrange("(j p) g -> p j g", p=P)[:, :, start : start + width], in_=result[:]
+            )
 
-        n = len(POST)
         for q, pieces in enumerate((THIRDS, HALVES)):
             for start, width in pieces:
-                add_two(nc.gpsimd, 0, q, start, width)
+                add_words(nc.gpsimd, 0, q, start, width)
+        for start, width in TURNED:
+            add_halfsums(nc.gpsimd, 0, start, width)
+            scale_turned(0, start, width)
+        add_words(nc.gpsimd, 1, 0, 0, 128)
 
-        def finish_total(i):
-            total(nc.vector, 1, i)
-            if POST[i][2]:
-                scale_by_turning(1, i)
-                interleave(i)
-
-        def finish(i):
-            quantize(i)
-            product(i)
-
-        def post_adds(i):
-            add_two(nc.vector, 1, 0, POST[i][0], POST[i][1])
-            add_two(nc.vector, 1, 1, POST[i][0], POST[i][1])
-
-        def first_total(i):
-            total(nc.gpsimd if i in GPSIMD_TOTALS else nc.vector, 0, i)
-            if POST[i][2]:
-                scale_by_turning(0, i)
-
-        first_total(0)
-        post_adds(0)
-        first_total(1)
-        finish_total(0)
-        post_adds(1)
-        first_total(2)
-        finish_total(1)
-        post_adds(2)
-        first_total(3)
-        finish_total(2)
-        post_adds(3)
-        first_total(4)
-        finish_total(3)
-        post_adds(4)
-        nc.scalar.activation(w_bf[:].rearrange("p (m t) -> p m t", t=PACK), w_raw[:].rearrange("p t m -> p m t"), COPY)
-        nc.vector.quantize_mx(out=w_codes[:].bitcast(FP8X4), scales=w_scales[:], in_=w_bf[:])
-        scale_in_place(3)
-        finish(0)
-        finish_total(4)
-        finish(1)
-        finish(3)
-        scale_in_place(4)
-        finish(2)
-        finish(4)
+        nc.scalar.activation(w_grouped[:].rearrange("p (m t) -> p m t", t=PACK), w_raw[:].rearrange("p t m -> p m t"), COPY)
+        nc.vector.quantize_mx(out=w_codes[:].bitcast(FP8X4), scales=w_scales[:], in_=w_grouped[:])
+        add_words(nc.vector, 1, 0, 128, 128)
+        add_words(nc.vector, 1, 1, 0, 256)
+        add_words(nc.vector, 1, 0, 256, 256)
+        add_words(nc.vector, 1, 1, 256, 256)
+        add_halfsums(nc.vector, 1, *TURNED[0])
+        scale_turned(1, *TURNED[0])
+        group_turned(*TURNED[0])
+        add_words(nc.vector, 1, 0, 512, 256)
+        add_words(nc.vector, 1, 1, 512, 256)
+        add_halfsums(nc.vector, 1, *TURNED[1])
+        scale_turned(1, *TURNED[1])
+        group_turned(*TURNED[1])
+        add_halfsums(nc.vector, 0, 512, 512)
+        add_words(nc.vector, 1, 0, 768, 256)
+        add_words(nc.vector, 1, 1, 768, 256)
+        add_halfsums(nc.vector, 1, 512, 256)
+        add_halfsums(nc.vector, 1, 768, 256)
+        scale_direct(*DIRECT[0])
+        quantize(*TURNED[0])
+        multiply(*TURNED[0], False)
+        scale_direct(*DIRECT[1])
+        quantize(*TURNED[1])
+        multiply(*TURNED[1], False)
+        quantize(*DIRECT[0])
+        multiply(*DIRECT[0], False)
+        scale_direct(*DIRECT[2])
+        quantize(*DIRECT[1])
+        multiply(*DIRECT[1], True)
+        quantize(*DIRECT[2])
+        multiply(*DIRECT[2], True)

@@ -22,9 +22,10 @@ COPY = mybir.ActivationFunctionType.Copy
 IDENTITY = mybir.ActivationFunctionType.Identity
 
 THIRDS = ((0, 384), (384, 384), (768, 256))
+EARLY = ((0, 384), (384, 640))
 HALVES = ((0, 512), (512, 512))
 TURNED = ((0, 256), (256, 256))
-DIRECT = ((512, 256), (768, 128), (896, 128))
+DIRECT = ((512, 256), (768, 256))
 
 
 def tile_attend_aq_bias_kernel(tc, cb, w, norm, bias, offs, out):
@@ -162,11 +163,13 @@ def tile_attend_aq_bias_kernel(tc, cb, w, norm, bias, offs, out):
         w_codes = keep.tile([P, M], U32, name="w_codes", align_bytes=64)
         w_scales = keep.tile([P, M], U8, name="w_scales", align_bytes=64)
 
-        def multiply(start, width, on_vector):
-            acc = psum.tile([P, M_TILES, width], F32, name="bank")
+        products = {}
+
+        def multiply(start, width):
             for j in range(M_TILES):
+                products[start, j] = psum.tile([P, width], F32, name="bank")
                 nc.tensor.matmul_mx(
-                    out=acc[:, j, :],
+                    out=products[start, j][:],
                     lhsT=w_codes[:, j * P : (j + 1) * P].bitcast(FP8X4),
                     lhsT_scale=w_scales[:, j * P : (j + 1) * P],
                     rhs=codes[start][:].bitcast(FP8X4),
@@ -174,29 +177,29 @@ def tile_attend_aq_bias_kernel(tc, cb, w, norm, bias, offs, out):
                     start=True,
                     stop=True,
                 )
-            result = keep.tile([P, M_TILES, width], F32, name=f"result{start}")
+
+        def finish(start, width, on_vector):
             for j in range(M_TILES):
-                if on_vector:
+                result = keep.tile([P, width], F32, name=f"result{start}_{j}")
+                if on_vector and j == 1:
                     nc.vector.tensor_scalar(
-                        out=result[:, j, :], in0=acc[:, j, :], scalar1=bias_cols[j][:], scalar2=None, op0=ADD
+                        out=result[:], in0=products[start, j][:], scalar1=bias_cols[j][:], scalar2=None, op0=ADD
                     )
                 else:
-                    nc.scalar.activation(result[:, j, :], acc[:, j, :], IDENTITY, bias=bias_cols[j][:])
-            nc.sync.dma_start(
-                out=out.rearrange("(j p) g -> p j g", p=P)[:, :, start : start + width], in_=result[:]
-            )
+                    nc.scalar.activation(result[:], products[start, j][:], IDENTITY, bias=bias_cols[j][:])
+                nc.sync.dma_start(out=out[j * P : (j + 1) * P, start : start + width], in_=result[:])
 
-        for q, pieces in enumerate((THIRDS, HALVES)):
+        for q, pieces in enumerate((EARLY, HALVES)):
             for start, width in pieces:
                 add_words(nc.gpsimd, 0, q, start, width)
+        add_halfsums(nc.gpsimd, 0, 0, 512)
         for start, width in TURNED:
-            add_halfsums(nc.gpsimd, 0, start, width)
             scale_turned(0, start, width)
-        add_words(nc.gpsimd, 1, 0, 0, 128)
+        add_words(nc.gpsimd, 1, 0, 0, 256)
+        add_halfsums(nc.gpsimd, 0, 512, 256)
 
         nc.scalar.activation(w_grouped[:].rearrange("p (m t) -> p m t", t=PACK), w_raw[:].rearrange("p t m -> p m t"), COPY)
         nc.vector.quantize_mx(out=w_codes[:].bitcast(FP8X4), scales=w_scales[:], in_=w_grouped[:])
-        add_words(nc.vector, 1, 0, 128, 128)
         add_words(nc.vector, 1, 1, 0, 256)
         add_words(nc.vector, 1, 0, 256, 256)
         add_words(nc.vector, 1, 1, 256, 256)
@@ -208,21 +211,22 @@ def tile_attend_aq_bias_kernel(tc, cb, w, norm, bias, offs, out):
         add_halfsums(nc.vector, 1, *TURNED[1])
         scale_turned(1, *TURNED[1])
         group_turned(*TURNED[1])
-        add_halfsums(nc.vector, 0, 512, 512)
         add_words(nc.vector, 1, 0, 768, 256)
         add_words(nc.vector, 1, 1, 768, 256)
         add_halfsums(nc.vector, 1, 512, 256)
+        add_halfsums(nc.vector, 0, 768, 256)
         add_halfsums(nc.vector, 1, 768, 256)
         scale_direct(*DIRECT[0])
         quantize(*TURNED[0])
-        multiply(*TURNED[0], False)
+        multiply(*TURNED[0])
+        finish(*TURNED[0], False)
         scale_direct(*DIRECT[1])
-        quantize(*TURNED[1])
-        multiply(*TURNED[1], False)
         quantize(*DIRECT[0])
-        multiply(*DIRECT[0], False)
-        scale_direct(*DIRECT[2])
+        multiply(*DIRECT[0])
+        quantize(*TURNED[1])
+        multiply(*TURNED[1])
         quantize(*DIRECT[1])
-        multiply(*DIRECT[1], True)
-        quantize(*DIRECT[2])
-        multiply(*DIRECT[2], True)
+        multiply(*DIRECT[1])
+        finish(*DIRECT[0], True)
+        finish(*TURNED[1], True)
+        finish(*DIRECT[1], True)

from contextlib import ExitStack

import concourse.mybir as mybir
from concourse.masks import make_identity

O, G, T, D, M = 4, 1024, 512, 512, 256
P = 128
PACK = 4
PAIRS = 2
M_TILES = M // P
FLOPS = 2 * D * M * G

F32 = mybir.dt.float32
BF16 = mybir.dt.bfloat16
U32 = mybir.dt.uint32
U16 = mybir.dt.uint16
U8 = mybir.dt.uint8
FP8X4 = mybir.dt.float8_e4m3fn_x4
ADD = mybir.AluOpType.add
MULT = mybir.AluOpType.mult
COPY = mybir.ActivationFunctionType.Copy
IDENTITY = mybir.ActivationFunctionType.Identity

THIRDS = ((0, 384), (384, 384), (768, 256))
EARLY = ((0, 384), (384, 640))
HALVES = ((0, 512), (512, 512))
TURNED = ((0, 256), (256, 256))
DIRECT = ((512, 256), (768, 256))


def tile_attend_aq_bias_kernel(tc, cb, w, norm, bias, offs, out):
    nc = tc.nc
    with ExitStack() as ctx:
        keep = ctx.enter_context(tc.tile_pool(name="keep", bufs=1))
        psum = ctx.enter_context(tc.psum_pool(name="psum", bufs=6))
        psum_back = ctx.enter_context(tc.psum_pool(name="psum_back", bufs=2))

        def pair_rows(o, h):
            return cb[o].rearrange("(p t) c -> p t c", t=PACK)[:, 2 * h : 2 * h + 2, :]

        offsets = keep.tile([P, O * G // 16], U16, name="offsets")
        tables = keep.tile([P, PAIRS * O * T * 2], BF16, name="tables")

        def table_at(o, h, slots):
            slot = PAIRS * O - 1 - (h * O + o)
            return tables[:, slot * 2 * T : (slot + slots) * 2 * T]

        half = T // 2
        raw_halves = [keep.tile([P, 2, half], F32, name=f"raw_half{i}") for i in range(2)]
        for i in range(2):
            nc.sync.dma_start(out=raw_halves[i][:], in_=pair_rows(0, 0)[:, :, i * half : (i + 1) * half])
        nc.sync.dma_start(offsets[:], offs)
        order = [(h, o) for h in range(PAIRS) for o in range(O)]
        raws = {}
        for h, o in order[1:]:
            raws[h, o] = keep.tile([P, 2, T], F32, name=f"raw{h}_{o}")
            nc.sync.dma_start(out=raws[h, o][:], in_=pair_rows(o, h))
        norm_rows = keep.tile([P, G], F32, name="norm_rows")
        nc.sync.dma_start(out=norm_rows[:], in_=norm)
        w_raw = keep.tile([P, PACK, M], F32, name="w_raw")
        nc.sync.dma_start(out=w_raw[:], in_=w.rearrange("(p t) m -> p t m", t=PACK))
        bias_cols = [keep.tile([P, 1], F32, name=f"bias{j}") for j in range(M_TILES)]
        for j in range(M_TILES):
            nc.sync.dma_start(out=bias_cols[j][:], in_=bias[j * P : (j + 1) * P, :])

        ident_f32 = keep.tile([P, P], F32, name="ident_f32")
        make_identity(nc, ident_f32[:])
        ident_bf16 = keep.tile([P, P], BF16, name="ident_bf16")
        make_identity(nc, ident_bf16[:])

        first = table_at(0, 0, 1).rearrange("p (c t) -> p c t", t=2)
        nc.scalar.activation(first[:, 0:half, :], raw_halves[0][:].rearrange("p t c -> p c t"), COPY)
        nc.vector.tensor_copy(first[:, half:T, :], raw_halves[1][:].rearrange("p t c -> p c t"))
        for h, o in order[1:]:
            nc.scalar.activation(
                table_at(o, h, 1).rearrange("p (c t) -> p c t", t=2), raws[h, o][:].rearrange("p t c -> p c t"), COPY
            )

        words = {(h, o): keep.tile([P, G], U32, name=f"words{h}_{o}") for h, o in order}

        def gather(h, o, start, width, slots):
            col = (o * G + start) // 16
            nc.vector.tensor_copy(
                words[h, o][:, start : start + width],
                table_at(o, h, slots).bitcast(U32).indirect(offsets[:, col : col + width // 16]),
            )

        for o, piece in ((0, 0), (0, 1), (1, 0), (0, 2), (1, 1), (1, 2)):
            gather(0, o, *THIRDS[piece], 1)
        gather(0, 2, 0, G, 3)
        for start, width in HALVES:
            gather(0, 3, start, width, 4)
        for o in range(O):
            gather(1, o, 0, G, 4)

        halfsums = {(h, q): keep.tile([P, 2 * G], F32, name=f"halfsum{h}_{q}") for h in range(PAIRS) for q in range(2)}
        sums = keep.tile([P, PAIRS, 2 * G], F32, name="sums")

        def add_words(engine, h, q, start, width):
            cols = slice(2 * start, 2 * (start + width))
            engine.tensor_tensor(
                halfsums[h, q][:, cols],
                words[h, 2 * q][:].bitcast(BF16)[:, cols],
                words[h, 2 * q + 1][:].bitcast(BF16)[:, cols],
                ADD,
            )

        def add_halfsums(engine, h, start, width):
            cols = slice(2 * start, 2 * (start + width))
            engine.tensor_tensor(sums[:, h, cols], halfsums[h, 0][:, cols], halfsums[h, 1][:, cols], ADD)

        norm_cols = keep.tile([P, G // P], F32, name="norm_cols")
        for part in range(2):
            turned = psum.tile([P, 4, P], F32, name="bank")
            for b in range(4):
                block = part * 4 + b
                nc.tensor.transpose(turned[:, b, :], norm_rows[:, block * P : (block + 1) * P], ident_f32[:])
            nc.scalar.copy(norm_cols[:, part * 4 : part * 4 + 4], turned[:, :, 0])

        backs = {}
        grouped = {}
        codes = {}
        scales = {}
        for start, width in TURNED + DIRECT:
            grouped[start] = keep.tile([P, width * PACK], BF16, name=f"grouped{start}", align_bytes=64)
            codes[start] = keep.tile([P, width], U32, name=f"codes{start}", align_bytes=64)
            scales[start] = keep.tile([P, width], U8, name=f"scales{start}", align_bytes=64)
        for start, width in TURNED:
            backs[start] = psum_back.tile([P, PACK, width], BF16, name="back")

        def scale_turned(h, start, width):
            blocks = width // P
            turned = psum.tile([P, blocks, 2, P], F32, name="bank")
            for b in range(blocks):
                for t in range(2):
                    first_col = 2 * (start + b * P) + t
                    nc.tensor.transpose(turned[:, b, t, :], sums[:, h, first_col : first_col + 2 * P - 1 : 2], ident_f32[:])
            scaled = keep.tile([P, blocks, 2, P], BF16, name=f"scaled{h}_{start}")
            for b in range(blocks):
                block = start // P + b
                nc.scalar.activation(scaled[:, b, :, :], turned[:, b, :, :], COPY, scale=norm_cols[:, block : block + 1])
            for b in range(blocks):
                for t in range(2):
                    nc.tensor.transpose(backs[start][:, 2 * h + t, b * P : (b + 1) * P], scaled[:, b, t, :], ident_bf16[:])

        def group_turned(start, width):
            nc.scalar.copy(
                grouped[start][:].rearrange("p (g t) -> p g t", t=PACK), backs[start][:].rearrange("p t g -> p g t")
            )

        def scale_direct(start, width):
            nc.vector.tensor_tensor(
                grouped[start][:].rearrange("p (g h t) -> p g h t", h=PAIRS, t=2),
                sums[:, :, 2 * start : 2 * (start + width)].rearrange("p h (g t) -> p g h t", t=2),
                norm_rows[:, start : start + width].unsqueeze(2).unsqueeze(3).to_broadcast([P, width, PAIRS, 2]),
                MULT,
            )

        def quantize(start, width):
            nc.vector.quantize_mx(out=codes[start][:].bitcast(FP8X4), scales=scales[start][:], in_=grouped[start][:])

        w_grouped = keep.tile([P, M * PACK], BF16, name="w_grouped", align_bytes=64)
        w_codes = keep.tile([P, M], U32, name="w_codes", align_bytes=64)
        w_scales = keep.tile([P, M], U8, name="w_scales", align_bytes=64)

        products = {}

        def multiply(start, width):
            for j in range(M_TILES):
                products[start, j] = psum.tile([P, width], F32, name="bank")
                nc.tensor.matmul_mx(
                    out=products[start, j][:],
                    lhsT=w_codes[:, j * P : (j + 1) * P].bitcast(FP8X4),
                    lhsT_scale=w_scales[:, j * P : (j + 1) * P],
                    rhs=codes[start][:].bitcast(FP8X4),
                    rhs_scale=scales[start][:],
                    start=True,
                    stop=True,
                )

        def finish(start, width, on_vector):
            for j in range(M_TILES):
                result = keep.tile([P, width], F32, name=f"result{start}_{j}")
                if on_vector and j == 1:
                    nc.vector.tensor_scalar(
                        out=result[:], in0=products[start, j][:], scalar1=bias_cols[j][:], scalar2=None, op0=ADD
                    )
                else:
                    nc.scalar.activation(result[:], products[start, j][:], IDENTITY, bias=bias_cols[j][:])
                nc.sync.dma_start(out=out[j * P : (j + 1) * P, start : start + width], in_=result[:])

        for q, pieces in enumerate((EARLY, HALVES)):
            for start, width in pieces:
                add_words(nc.gpsimd, 0, q, start, width)
        add_halfsums(nc.gpsimd, 0, 0, 512)
        for start, width in TURNED:
            scale_turned(0, start, width)
        add_words(nc.gpsimd, 1, 0, 0, 256)
        add_halfsums(nc.gpsimd, 0, 512, 256)

        nc.scalar.activation(w_grouped[:].rearrange("p (m t) -> p m t", t=PACK), w_raw[:].rearrange("p t m -> p m t"), COPY)
        nc.vector.quantize_mx(out=w_codes[:].bitcast(FP8X4), scales=w_scales[:], in_=w_grouped[:])
        add_words(nc.vector, 1, 1, 0, 256)
        add_words(nc.vector, 1, 0, 256, 256)
        add_words(nc.vector, 1, 1, 256, 256)
        add_halfsums(nc.vector, 1, *TURNED[0])
        scale_turned(1, *TURNED[0])
        group_turned(*TURNED[0])
        add_words(nc.vector, 1, 0, 512, 256)
        add_words(nc.vector, 1, 1, 512, 256)
        add_halfsums(nc.vector, 1, *TURNED[1])
        scale_turned(1, *TURNED[1])
        group_turned(*TURNED[1])
        add_words(nc.vector, 1, 0, 768, 256)
        add_words(nc.vector, 1, 1, 768, 256)
        add_halfsums(nc.vector, 1, 512, 256)
        add_halfsums(nc.vector, 0, 768, 256)
        add_halfsums(nc.vector, 1, 768, 256)
        scale_direct(*DIRECT[0])
        quantize(*TURNED[0])
        multiply(*TURNED[0])
        finish(*TURNED[0], False)
        scale_direct(*DIRECT[1])
        quantize(*DIRECT[0])
        multiply(*DIRECT[0])
        quantize(*TURNED[1])
        multiply(*TURNED[1])
        quantize(*DIRECT[1])
        multiply(*DIRECT[1])
        finish(*DIRECT[0], True)
        finish(*TURNED[1], True)
        finish(*DIRECT[1], True)
